import numpy as np
import ml_dtypes


def mxq(x, axis, fmt="e4m3"):
    dtype, down = {"e4m3": (ml_dtypes.float8_e4m3fn, 7), "e5m2": (ml_dtypes.float8_e5m2, 14)}[fmt]
    v = np.moveaxis(np.asarray(x, np.float32).astype(ml_dtypes.bfloat16).astype(np.float64), axis, -1)
    blocks = v.reshape(v.shape[:-1] + (-1, 32))
    amax = np.abs(blocks).max(-1, keepdims=True)
    byte = np.maximum(np.where(amax > 0, np.frexp(amax)[1] - 1 + 127, 0) - down, 1)
    scale = np.exp2(byte - 127.0)
    codes = (blocks / scale).astype(np.float32).astype(dtype).astype(np.float64)
    return np.moveaxis((codes * scale).reshape(v.shape), -1, axis)


WIDE = False


def mx_kscale(k, group=512):
    if not WIDE:
        return np.ones(k)
    levels = np.array([18, -18])
    if group != 512:
        return np.exp2(np.random.permutation(np.resize(levels, k // group))).repeat(group)
    if k % 512:
        return np.exp2(np.random.permutation(np.resize(levels, k // 32))).repeat(32)
    a = np.empty((k // 512, 16))
    for p in range(k // 512):
        a[p, :8] = np.random.permutation(np.resize(levels, 8))
        for g in range(8):
            far = levels[np.abs(levels - a[p, g]) >= 10]
            a[p, g + 8] = far[np.random.randint(len(far))]
    return np.exp2(a.ravel()).repeat(32)


def f64(x):
    return np.asarray(x).astype(np.float64)


E2M1 = np.array([0.0, 0.5, 1.0, 1.5, 2.0, 3.0, 4.0, 6.0, -0.0, -0.5, -1.0, -1.5, -2.0, -3.0, -4.0, -6.0])


def pack_group(w):
    k, n = w.shape
    w = f64(np.asarray(w, np.float32).astype(ml_dtypes.bfloat16)).reshape(k // 32, 32, n)
    amax = np.abs(w).max(1)
    mant, ex = np.frexp(amax / 6.0)
    byte = np.clip(np.where(amax > 0, np.where(mant > 0.5, ex, ex - 1) + 127, 1), 1, 254)
    scaled = (w * np.exp2(127.0 - byte)[:, None, :]).reshape(k, n).astype(np.float32)
    c = np.ascontiguousarray(scaled.reshape(k // 4, 4, n).transpose(0, 2, 1)).astype(ml_dtypes.float4_e2m1fn).view(np.uint8) & 0xF
    return np.ascontiguousarray((c[..., 0::2] | (c[..., 1::2] << 4)).reshape(k // 4, 2 * n)), byte.astype(np.uint8)


def unpack_group(words, scales):
    p, n = words.shape[0], scales.shape[1]
    words = np.ascontiguousarray(words).reshape(p, n, 2)
    nib = np.empty((p, n, 4), np.uint8)
    nib[..., 0::2] = words & 0xF
    nib[..., 1::2] = words >> 4
    return E2M1[nib].transpose(0, 2, 1).reshape(4 * p, n) * np.repeat(np.exp2(scales.astype(np.float64) - 127.0), 32, axis=0)


G, D, M, F, O, N = 4, 128, 128, 128, 128, 512


def sgn(shape):
    return np.random.uniform(0.5, 2.0, shape) * np.where(np.random.standard_normal(shape) < 0, -1.0, 1.0)


def setup_inputs():
    n = np.random.standard_normal
    s_d = mx_kscale(D, 0)
    s_f = mx_kscale(F, 0)
    w_ = [pack_group(w) for w in n((G, D, M)) / np.sqrt(D) / s_d[:, None]]
    v_ = [pack_group(w) for w in n((G, F, O)) / np.sqrt(F) / s_f[:, None]]
    return {
        "x": (n((G, D, N)) * s_d[:, None]).astype(np.float32),
        "w_words": np.stack([w[0] for w in w_]),
        "w_scales": np.stack([w[1] for w in w_]),
        "hs": (sgn((G, M, 1)) * np.tile(s_f.reshape(F // G, G).T, (1, G))[:, :, None]).astype(np.float32),
        "v_words": np.stack([w[0] for w in v_]),
        "v_scales": np.stack([w[1] for w in v_]),
    }


def reference(x, w_words, w_scales, hs, v_words, v_scales):
    w = np.stack([unpack_group(w_words[g], w_scales[g]) for g in range(G)])
    xq = mxq(f64(x), 1, "e4m3")
    z = w.transpose(0, 2, 1) @ xq
    h = np.maximum(z, 0.0) * f64(hs)
    u = h.reshape(G * M, N).reshape(G, M, N).transpose(1, 0, 2).reshape(G, M, N)
    v = np.stack([unpack_group(v_words[g], v_scales[g]) for g in range(G)])
    uq = mxq(u, 1, "e4m3")
    a = v.transpose(0, 2, 1) @ uq
    return a

@@ -1,0 +1,138 @@
+from contextlib import ExitStack
+
+import concourse.mybir as mybir
+
+G, D, M, F, O, N = 4, 128, 128, 128, 128, 512
+FLOPS = 2 * G * (D * M + F * O) * N
+
+F32 = mybir.dt.float32
+BF16 = mybir.dt.bfloat16
+I32 = mybir.dt.int32
+U32 = mybir.dt.uint32
+U8 = mybir.dt.uint8
+FP8X4 = mybir.dt.float8_e4m3fn_x4
+FP4X4 = mybir.dt.float4_e2m1fn_x4
+ALU = mybir.AluOpType
+ACT = mybir.ActivationFunctionType
+
+P = 128
+ROWS = 32
+PACK = 4
+HALF = N // 2
+RUN = 4
+SPLIT = 160
+
+
+def tile_rows_monarch_kernel(tc, x, w_words, w_scales, hs, v_words, v_scales, out):
+    nc = tc.nc
+    with ExitStack() as ctx:
+        sb = ctx.enter_context(tc.tile_pool(name="sb", bufs=1))
+        ps = ctx.enter_context(tc.psum_pool(name="ps", bufs=1))
+        ctx.enter_context(tc.manual_schedule())
+
+        raw = [sb.tile([P, PACK, HALF], F32, name="raw%d" % c, align_bytes=64) for c in range(2)]
+        xg = [sb.tile([P, HALF, PACK], BF16, name="xg%d" % c, align_bytes=64) for c in range(2)]
+        hb = [sb.tile([P, G, HALF], BF16, name="hb%d" % c, align_bytes=64) for c in range(2)]
+        ug = [sb.tile([P, HALF, PACK], BF16, name="ug%d" % c, align_bytes=64) for c in range(2)]
+        res = [[sb.tile([P, HALF], F32, name="res%d_%d" % (c, g), align_bytes=64) for g in range(G)] for c in range(2)]
+        codes = sb.tile([P, 5 * HALF], U32, name="codes", align_bytes=256)
+        scales = sb.tile([P, 5 * HALF], U8, name="scales", align_bytes=256)
+        ww = sb.tile([P, 2 * M], U8, name="ww", align_bytes=256)
+        vw = sb.tile([P, 2 * O], U8, name="vw", align_bytes=256)
+        wsc = sb.tile([P, M], U8, name="wsc", align_bytes=64)
+        vsc = sb.tile([P, O], U8, name="vsc", align_bytes=64)
+        hs_rows = sb.tile([P, G, ROWS], F32, name="hs_rows", align_bytes=64)
+        hs_cols = sb.tile([P, G, ROWS], F32, name="hs_cols", align_bytes=64)
+        hs_abs = sb.tile([P, G], F32, name="hs_abs")
+        hs_half_sign = sb.tile([P, G], F32, name="hs_half_sign")
+        banks = [[ps.tile([P, N], F32, name="bank%d_%d" % (c, g)) for g in range(G)] for c in range(2)]
+
+        x_rows = x.rearrange("g (p j) n -> (g p) j n", j=PACK)
+
+        nc.vector.memset(hs_rows[:], 0.0)
+        nc.vector.memset(wsc[:].bitcast(U32), 0)
+        nc.vector.memset(vsc[:].bitcast(U32), 0)
+        nc.vector.memset(codes[:, 0:HALF], 0)
+        nc.vector.memset(scales[:, 0:HALF].bitcast(U32), 0)
+
+        nc.sync.dma_start(out=raw[0][:], in_=x_rows[:, :, 0:HALF])
+        nc.sync.dma_start(out=ww[:].bitcast(I32), in_=w_words.rearrange("g p c -> (g p) c").bitcast(I32))
+        nc.scalar.dma_start(out=hs_rows[0:P:ROWS, :, :], in_=hs.rearrange("g (a b) o -> a g (b o)", b=ROWS))
+        for g in range(G):
+            nc.scalar.dma_start(out=wsc[ROWS * g:ROWS * g + 4, :].bitcast(I32), in_=w_scales[g].bitcast(I32))
+        nc.sync.dma_start(out=raw[1][:], in_=x_rows[:, :, HALF:N])
+        nc.sync.dma_start(out=vw[:].bitcast(I32), in_=v_words.rearrange("g p c -> (g p) c").bitcast(I32))
+        for g in range(G):
+            nc.sync.dma_start(out=vsc[ROWS * g:ROWS * g + 4, :].bitcast(I32), in_=v_scales[g].bitcast(I32))
+
+        nc.vector.transpose(hs_cols[:].rearrange("p g b -> p (g b)"), hs_rows[:].rearrange("p g b -> p (g b)"))
+        nc.vector.scalar_tensor_tensor(out=hs_abs[:], in0=hs_cols[:, :, 0], scalar=-1.0, in1=hs_cols[:, :, 0],
+                                       op0=ALU.mult, op1=ALU.max)
+        nc.vector.tensor_scalar(out=hs_half_sign[:], in0=hs_cols[:, :, 0], scalar1=0.0, scalar2=0.5,
+                                op0=ALU.is_ge, op1=ALU.subtract)
+
+        def views(dst, src, lo, hi):
+            return (dst[:, lo:hi, :].rearrange("p (c i) j -> p c j i", i=RUN),
+                    src[:, :, lo:hi].rearrange("p j (c i) -> p c j i", i=RUN))
+
+        def interleave(dst, src):
+            o, i = views(dst, src, 0, SPLIT)
+            nc.vector.tensor_copy(out=o, in_=i)
+            o, i = views(dst, src, SPLIT, HALF)
+            nc.scalar.copy(out=o, in_=i)
+
+        def quantize(src, slot):
+            cols = slice(slot * HALF, (slot + 1) * HALF)
+            nc.vector.quantize_mx(out=codes[:, cols].bitcast(FP8X4), scales=scales[:, cols],
+                                  in_=src[:].rearrange("p n j -> p (n j)"))
+
+        def multiply(words, wscales, slot, c):
+            cols = slice((slot - 1) * HALF, (slot + 1) * HALF)
+            for g in range(G):
+                rows = slice(ROWS * g, ROWS * (g + 1))
+                nc.tensor.matmul_mx(out=banks[c][g][:], lhsT=words[rows, :].bitcast(FP4X4),
+                                    lhsT_scale=wscales[rows, :], rhs=codes[rows, cols].bitcast(FP8X4),
+                                    rhs_scale=scales[rows, cols], start=True, stop=True)
+
+        def hidden(c, on_vector):
+            for g in range(G):
+                z = banks[c][g][:, HALF:N]
+                if g < on_vector:
+                    nc.vector.tensor_scalar(out=hb[c][:, g, :], in0=z, scalar1=0.0, scalar2=hs_cols[:, g, 0:1],
+                                            op0=ALU.max, op1=ALU.mult)
+                else:
+                    nc.scalar.activation(out=hb[c][:, g, :], in_=z, func=ACT.Relu, scale=hs_abs[:, g:g + 1])
+            for g in range(on_vector, G):
+                nc.vector.tensor_scalar(out=hb[c][:, g, :], in0=hb[c][:, g, :], scalar1=hs_half_sign[:, g:g + 1],
+                                        scalar2=2.0, op0=ALU.mult, op1=ALU.mult)
+
+        def result(c, on_scalar):
+            for g in range(G):
+                a = banks[c][g][:, HALF:N]
+                if g < on_scalar:
+                    nc.scalar.copy(out=res[c][g][:], in_=a)
+                else:
+                    nc.vector.tensor_copy(out=res[c][g][:], in_=a)
+
+        def store(c, order):
+            for g in order:
+                nc.sync.dma_start(out=out[g, :, c * HALF:(c + 1) * HALF], in_=res[c][g][:])
+
+        interleave(xg[0], raw[0])
+        quantize(xg[0], 1)
+        multiply(ww, wsc, 1, 0)
+        interleave(xg[1], raw[1])
+        quantize(xg[1], 2)
+        multiply(ww, wsc, 2, 1)
+        hidden(0, 2)
+        interleave(ug[0], hb[0])
+        quantize(ug[0], 3)
+        multiply(vw, vsc, 3, 0)
+        hidden(1, 1)
+        interleave(ug[1], hb[1])
+        quantize(ug[1], 4)
+        multiply(vw, vsc, 4, 1)
+        result(0, 3)
+        store(0, [0, 1, 3, 2])
+        result(1, 2)
+        store(1, [0, 2, 1, 3])

@@ -20,7 +20,8 @@ ROWS = 32
 PACK = 4
 HALF = N // 2
 RUN = 4
-SPLIT = 160
+X_SPLIT = 144
+U_SPLIT = 128
 
 
 def tile_rows_monarch_kernel(tc, x, w_words, w_scales, hs, v_words, v_scales, out):
@@ -56,30 +57,19 @@ def tile_rows_monarch_kernel(tc, x, w_words, w_scales, hs, v_words, v_scales, ou
         nc.vector.memset(scales[:, 0:HALF].bitcast(U32), 0)
 
         nc.sync.dma_start(out=raw[0][:], in_=x_rows[:, :, 0:HALF])
+        nc.sync.dma_start(out=hs_rows[0:P:ROWS, :, :], in_=hs.rearrange("g (a b) o -> a g (b o)", b=ROWS))
         nc.sync.dma_start(out=ww[:].bitcast(I32), in_=w_words.rearrange("g p c -> (g p) c").bitcast(I32))
-        nc.scalar.dma_start(out=hs_rows[0:P:ROWS, :, :], in_=hs.rearrange("g (a b) o -> a g (b o)", b=ROWS))
         for g in range(G):
-            nc.scalar.dma_start(out=wsc[ROWS * g:ROWS * g + 4, :].bitcast(I32), in_=w_scales[g].bitcast(I32))
+            nc.sync.dma_start(out=wsc[ROWS * g:ROWS * g + 4, :].bitcast(I32), in_=w_scales[g].bitcast(I32))
         nc.sync.dma_start(out=raw[1][:], in_=x_rows[:, :, HALF:N])
         nc.sync.dma_start(out=vw[:].bitcast(I32), in_=v_words.rearrange("g p c -> (g p) c").bitcast(I32))
         for g in range(G):
             nc.sync.dma_start(out=vsc[ROWS * g:ROWS * g + 4, :].bitcast(I32), in_=v_scales[g].bitcast(I32))
 
-        nc.vector.transpose(hs_cols[:].rearrange("p g b -> p (g b)"), hs_rows[:].rearrange("p g b -> p (g b)"))
-        nc.vector.scalar_tensor_tensor(out=hs_abs[:], in0=hs_cols[:, :, 0], scalar=-1.0, in1=hs_cols[:, :, 0],
-                                       op0=ALU.mult, op1=ALU.max)
-        nc.vector.tensor_scalar(out=hs_half_sign[:], in0=hs_cols[:, :, 0], scalar1=0.0, scalar2=0.5,
-                                op0=ALU.is_ge, op1=ALU.subtract)
-
-        def views(dst, src, lo, hi):
-            return (dst[:, lo:hi, :].rearrange("p (c i) j -> p c j i", i=RUN),
-                    src[:, :, lo:hi].rearrange("p j (c i) -> p c j i", i=RUN))
-
-        def interleave(dst, src):
-            o, i = views(dst, src, 0, SPLIT)
-            nc.vector.tensor_copy(out=o, in_=i)
-            o, i = views(dst, src, SPLIT, HALF)
-            nc.scalar.copy(out=o, in_=i)
+        def interleave(dst, src, split):
+            for copy, lo, hi in ((nc.vector.tensor_copy, 0, split), (nc.scalar.copy, split, HALF)):
+                copy(out=dst[:, lo:hi, :].rearrange("p (c i) j -> p c j i", i=RUN),
+                     in_=src[:, :, lo:hi].rearrange("p j (c i) -> p c j i", i=RUN))
 
         def quantize(src, slot):
             cols = slice(slot * HALF, (slot + 1) * HALF)
@@ -94,45 +84,55 @@ def tile_rows_monarch_kernel(tc, x, w_words, w_scales, hs, v_words, v_scales, ou
                                     lhsT_scale=wscales[rows, :], rhs=codes[rows, cols].bitcast(FP8X4),
                                     rhs_scale=scales[rows, cols], start=True, stop=True)
 
-        def hidden(c, on_vector):
-            for g in range(G):
-                z = banks[c][g][:, HALF:N]
-                if g < on_vector:
-                    nc.vector.tensor_scalar(out=hb[c][:, g, :], in0=z, scalar1=0.0, scalar2=hs_cols[:, g, 0:1],
-                                            op0=ALU.max, op1=ALU.mult)
-                else:
-                    nc.scalar.activation(out=hb[c][:, g, :], in_=z, func=ACT.Relu, scale=hs_abs[:, g:g + 1])
-            for g in range(on_vector, G):
-                nc.vector.tensor_scalar(out=hb[c][:, g, :], in0=hb[c][:, g, :], scalar1=hs_half_sign[:, g:g + 1],
-                                        scalar2=2.0, op0=ALU.mult, op1=ALU.mult)
+        def hidden_v(c, g):
+            nc.vector.tensor_scalar(out=hb[c][:, g, :], in0=banks[c][g][:, HALF:N], scalar1=0.0,
+                                    scalar2=hs_cols[:, g, 0:1], op0=ALU.max, op1=ALU.mult)
 
-        def result(c, on_scalar):
-            for g in range(G):
-                a = banks[c][g][:, HALF:N]
-                if g < on_scalar:
-                    nc.scalar.copy(out=res[c][g][:], in_=a)
-                else:
-                    nc.vector.tensor_copy(out=res[c][g][:], in_=a)
+        def hidden_s(c, g):
+            nc.scalar.activation(out=hb[c][:, g, :], in_=banks[c][g][:, HALF:N], func=ACT.Relu,
+                                 scale=hs_abs[:, g:g + 1])
 
-        def store(c, order):
-            for g in order:
-                nc.sync.dma_start(out=out[g, :, c * HALF:(c + 1) * HALF], in_=res[c][g][:])
+        def sign_v(c, g):
+            nc.vector.tensor_scalar(out=hb[c][:, g, :], in0=hb[c][:, g, :], scalar1=hs_half_sign[:, g:g + 1],
+                                    scalar2=2.0, op0=ALU.mult, op1=ALU.mult)
 
-        interleave(xg[0], raw[0])
+        def result(c, g, copy):
+            copy(out=res[c][g][:], in_=banks[c][g][:, HALF:N])
+            nc.sync.dma_start(out=out[g, :, c * HALF:(c + 1) * HALF], in_=res[c][g][:])
+
+        interleave(xg[0], raw[0], X_SPLIT)
+        nc.vector.transpose(hs_cols[:].rearrange("p g b -> p (g b)"), hs_rows[:].rearrange("p g b -> p (g b)"))
         quantize(xg[0], 1)
         multiply(ww, wsc, 1, 0)
-        interleave(xg[1], raw[1])
+        nc.vector.scalar_tensor_tensor(out=hs_abs[:], in0=hs_cols[:, :, 0], scalar=-1.0, in1=hs_cols[:, :, 0],
+                                       op0=ALU.mult, op1=ALU.max)
+        nc.vector.tensor_scalar(out=hs_half_sign[:], in0=hs_cols[:, :, 0], scalar1=0.0, scalar2=0.5,
+                                op0=ALU.is_ge, op1=ALU.subtract)
+        interleave(xg[1], raw[1], X_SPLIT)
         quantize(xg[1], 2)
         multiply(ww, wsc, 2, 1)
-        hidden(0, 2)
-        interleave(ug[0], hb[0])
+
+        hidden_s(0, 0)
+        hidden_s(0, 1)
+        hidden_v(0, 2)
+        sign_v(0, 0)
+        sign_v(0, 1)
+        hidden_v(0, 3)
+        hidden_v(1, 0)
+        interleave(ug[0], hb[0], U_SPLIT)
+        hidden_v(1, 1)
         quantize(ug[0], 3)
         multiply(vw, vsc, 3, 0)
-        hidden(1, 1)
-        interleave(ug[1], hb[1])
+        hidden_s(1, 2)
+        hidden_s(1, 3)
+        sign_v(1, 2)
+        sign_v(1, 3)
+        interleave(ug[1], hb[1], U_SPLIT)
         quantize(ug[1], 4)
         multiply(vw, vsc, 4, 1)
-        result(0, 3)
-        store(0, [0, 1, 3, 2])
-        result(1, 2)
-        store(1, [0, 2, 1, 3])
+        result(0, 0, nc.scalar.copy)
+        result(0, 1, nc.scalar.copy)
+        result(0, 3, nc.vector.tensor_copy)
+        result(0, 2, nc.scalar.copy)
+        for g in range(G):
+            result(1, g, nc.vector.tensor_copy if g % 2 else nc.scalar.copy)

@@ -21,7 +21,8 @@ PACK = 4
 HALF = N // 2
 RUN = 4
 X_SPLIT = 144
-U_SPLIT = 128
+UA_SPLIT = 48
+UB_SPLIT = 144
 
 
 def tile_rows_monarch_kernel(tc, x, w_words, w_scales, hs, v_words, v_scales, out):
@@ -112,27 +113,22 @@ def tile_rows_monarch_kernel(tc, x, w_words, w_scales, hs, v_words, v_scales, ou
         quantize(xg[1], 2)
         multiply(ww, wsc, 2, 1)
 
-        hidden_s(0, 0)
-        hidden_s(0, 1)
-        hidden_v(0, 2)
-        sign_v(0, 0)
-        sign_v(0, 1)
-        hidden_v(0, 3)
+        for g in range(G):
+            if g % 2:
+                hidden_v(0, g)
+            else:
+                hidden_s(0, g)
+        for g in range(0, G, 2):
+            sign_v(0, g)
         hidden_v(1, 0)
-        interleave(ug[0], hb[0], U_SPLIT)
-        hidden_v(1, 1)
+        interleave(ug[0], hb[0], UA_SPLIT)
+        for g in range(1, G):
+            hidden_v(1, g)
         quantize(ug[0], 3)
         multiply(vw, vsc, 3, 0)
-        hidden_s(1, 2)
-        hidden_s(1, 3)
-        sign_v(1, 2)
-        sign_v(1, 3)
-        interleave(ug[1], hb[1], U_SPLIT)
+        interleave(ug[1], hb[1], UB_SPLIT)
         quantize(ug[1], 4)
         multiply(vw, vsc, 4, 1)
-        result(0, 0, nc.scalar.copy)
-        result(0, 1, nc.scalar.copy)
-        result(0, 3, nc.vector.tensor_copy)
-        result(0, 2, nc.scalar.copy)
-        for g in range(G):
-            result(1, g, nc.vector.tensor_copy if g % 2 else nc.scalar.copy)
+        for c in range(2):
+            for g in range(G):
+                result(c, g, nc.vector.tensor_copy if g % 2 else nc.scalar.copy)

from contextlib import ExitStack

import concourse.mybir as mybir

G, D, M, F, O, N = 4, 128, 128, 128, 128, 512
FLOPS = 2 * G * (D * M + F * O) * N

F32 = mybir.dt.float32
BF16 = mybir.dt.bfloat16
I32 = mybir.dt.int32
U32 = mybir.dt.uint32
U8 = mybir.dt.uint8
FP8X4 = mybir.dt.float8_e4m3fn_x4
FP4X4 = mybir.dt.float4_e2m1fn_x4
ALU = mybir.AluOpType
ACT = mybir.ActivationFunctionType

P = 128
ROWS = 32
PACK = 4
HALF = N // 2
RUN = 4
X_SPLIT = 144
UA_SPLIT = 48
UB_SPLIT = 144


def tile_rows_monarch_kernel(tc, x, w_words, w_scales, hs, v_words, v_scales, out):
    nc = tc.nc
    with ExitStack() as ctx:
        sb = ctx.enter_context(tc.tile_pool(name="sb", bufs=1))
        ps = ctx.enter_context(tc.psum_pool(name="ps", bufs=1))
        ctx.enter_context(tc.manual_schedule())

        raw = [sb.tile([P, PACK, HALF], F32, name="raw%d" % c, align_bytes=64) for c in range(2)]
        xg = [sb.tile([P, HALF, PACK], BF16, name="xg%d" % c, align_bytes=64) for c in range(2)]
        hb = [sb.tile([P, G, HALF], BF16, name="hb%d" % c, align_bytes=64) for c in range(2)]
        ug = [sb.tile([P, HALF, PACK], BF16, name="ug%d" % c, align_bytes=64) for c in range(2)]
        res = [[sb.tile([P, HALF], F32, name="res%d_%d" % (c, g), align_bytes=64) for g in range(G)] for c in range(2)]
        codes = sb.tile([P, 5 * HALF], U32, name="codes", align_bytes=256)
        scales = sb.tile([P, 5 * HALF], U8, name="scales", align_bytes=256)
        ww = sb.tile([P, 2 * M], U8, name="ww", align_bytes=256)
        vw = sb.tile([P, 2 * O], U8, name="vw", align_bytes=256)
        wsc = sb.tile([P, M], U8, name="wsc", align_bytes=64)
        vsc = sb.tile([P, O], U8, name="vsc", align_bytes=64)
        hs_rows = sb.tile([P, G, ROWS], F32, name="hs_rows", align_bytes=64)
        hs_cols = sb.tile([P, G, ROWS], F32, name="hs_cols", align_bytes=64)
        hs_abs = sb.tile([P, G], F32, name="hs_abs")
        hs_half_sign = sb.tile([P, G], F32, name="hs_half_sign")
        banks = [[ps.tile([P, N], F32, name="bank%d_%d" % (c, g)) for g in range(G)] for c in range(2)]

        x_rows = x.rearrange("g (p j) n -> (g p) j n", j=PACK)

        nc.vector.memset(hs_rows[:], 0.0)
        nc.vector.memset(wsc[:].bitcast(U32), 0)
        nc.vector.memset(vsc[:].bitcast(U32), 0)
        nc.vector.memset(codes[:, 0:HALF], 0)
        nc.vector.memset(scales[:, 0:HALF].bitcast(U32), 0)

        nc.sync.dma_start(out=raw[0][:], in_=x_rows[:, :, 0:HALF])
        nc.sync.dma_start(out=hs_rows[0:P:ROWS, :, :], in_=hs.rearrange("g (a b) o -> a g (b o)", b=ROWS))
        nc.sync.dma_start(out=ww[:].bitcast(I32), in_=w_words.rearrange("g p c -> (g p) c").bitcast(I32))
        for g in range(G):
            nc.sync.dma_start(out=wsc[ROWS * g:ROWS * g + 4, :].bitcast(I32), in_=w_scales[g].bitcast(I32))
        nc.sync.dma_start(out=raw[1][:], in_=x_rows[:, :, HALF:N])
        nc.sync.dma_start(out=vw[:].bitcast(I32), in_=v_words.rearrange("g p c -> (g p) c").bitcast(I32))
        for g in range(G):
            nc.sync.dma_start(out=vsc[ROWS * g:ROWS * g + 4, :].bitcast(I32), in_=v_scales[g].bitcast(I32))

        def interleave(dst, src, split):
            for copy, lo, hi in ((nc.vector.tensor_copy, 0, split), (nc.scalar.copy, split, HALF)):
                copy(out=dst[:, lo:hi, :].rearrange("p (c i) j -> p c j i", i=RUN),
                     in_=src[:, :, lo:hi].rearrange("p j (c i) -> p c j i", i=RUN))

        def quantize(src, slot):
            cols = slice(slot * HALF, (slot + 1) * HALF)
            nc.vector.quantize_mx(out=codes[:, cols].bitcast(FP8X4), scales=scales[:, cols],
                                  in_=src[:].rearrange("p n j -> p (n j)"))

        def multiply(words, wscales, slot, c):
            cols = slice((slot - 1) * HALF, (slot + 1) * HALF)
            for g in range(G):
                rows = slice(ROWS * g, ROWS * (g + 1))
                nc.tensor.matmul_mx(out=banks[c][g][:], lhsT=words[rows, :].bitcast(FP4X4),
                                    lhsT_scale=wscales[rows, :], rhs=codes[rows, cols].bitcast(FP8X4),
                                    rhs_scale=scales[rows, cols], start=True, stop=True)

        def hidden_v(c, g):
            nc.vector.tensor_scalar(out=hb[c][:, g, :], in0=banks[c][g][:, HALF:N], scalar1=0.0,
                                    scalar2=hs_cols[:, g, 0:1], op0=ALU.max, op1=ALU.mult)

        def hidden_s(c, g):
            nc.scalar.activation(out=hb[c][:, g, :], in_=banks[c][g][:, HALF:N], func=ACT.Relu,
                                 scale=hs_abs[:, g:g + 1])

        def sign_v(c, g):
            nc.vector.tensor_scalar(out=hb[c][:, g, :], in0=hb[c][:, g, :], scalar1=hs_half_sign[:, g:g + 1],
                                    scalar2=2.0, op0=ALU.mult, op1=ALU.mult)

        def result(c, g, copy):
            copy(out=res[c][g][:], in_=banks[c][g][:, HALF:N])
            nc.sync.dma_start(out=out[g, :, c * HALF:(c + 1) * HALF], in_=res[c][g][:])

        interleave(xg[0], raw[0], X_SPLIT)
        nc.vector.transpose(hs_cols[:].rearrange("p g b -> p (g b)"), hs_rows[:].rearrange("p g b -> p (g b)"))
        quantize(xg[0], 1)
        multiply(ww, wsc, 1, 0)
        nc.vector.scalar_tensor_tensor(out=hs_abs[:], in0=hs_cols[:, :, 0], scalar=-1.0, in1=hs_cols[:, :, 0],
                                       op0=ALU.mult, op1=ALU.max)
        nc.vector.tensor_scalar(out=hs_half_sign[:], in0=hs_cols[:, :, 0], scalar1=0.0, scalar2=0.5,
                                op0=ALU.is_ge, op1=ALU.subtract)
        interleave(xg[1], raw[1], X_SPLIT)
        quantize(xg[1], 2)
        multiply(ww, wsc, 2, 1)

        for g in range(G):
            if g % 2:
                hidden_v(0, g)
            else:
                hidden_s(0, g)
        for g in range(0, G, 2):
            sign_v(0, g)
        hidden_v(1, 0)
        interleave(ug[0], hb[0], UA_SPLIT)
        for g in range(1, G):
            hidden_v(1, g)
        quantize(ug[0], 3)
        multiply(vw, vsc, 3, 0)
        interleave(ug[1], hb[1], UB_SPLIT)
        quantize(ug[1], 4)
        multiply(vw, vsc, 4, 1)
        for c in range(2):
            for g in range(G):
                result(c, g, nc.vector.tensor_copy if g % 2 else nc.scalar.copy)
